import numpy as np
import ml_dtypes


def mxq(x, axis, fmt="e4m3"):
    dtype, down = {"e4m3": (ml_dtypes.float8_e4m3fn, 7), "e5m2": (ml_dtypes.float8_e5m2, 14)}[fmt]
    v = np.moveaxis(np.asarray(x, np.float32).astype(ml_dtypes.bfloat16).astype(np.float64), axis, -1)
    blocks = v.reshape(v.shape[:-1] + (-1, 32))
    amax = np.abs(blocks).max(-1, keepdims=True)
    byte = np.maximum(np.where(amax > 0, np.frexp(amax)[1] - 1 + 127, 0) - down, 1)
    scale = np.exp2(byte - 127.0)
    codes = (blocks / scale).astype(np.float32).astype(dtype).astype(np.float64)
    return np.moveaxis((codes * scale).reshape(v.shape), -1, axis)


WIDE = False


def mx_kscale(k):
    if not WIDE:
        return np.ones(k)
    levels = np.array([10, -10, 5, -5, 0])
    if k % 512:
        return np.exp2(np.random.permutation(np.resize(levels, k // 32))).repeat(32)
    a = np.empty((k // 512, 16))
    for p in range(k // 512):
        a[p, :8] = np.random.permutation(np.resize(levels, 8))
        for g in range(8):
            far = levels[np.abs(levels - a[p, g]) >= 10]
            a[p, g + 8] = far[np.random.randint(len(far))]
    return np.exp2(a.ravel()).repeat(32)


def f64(x):
    return np.asarray(x).astype(np.float64)


def striped(idx):
    return np.tile(idx.reshape(-1, 16).T, (8, 1)).astype(np.uint16)


def unstriped(offs):
    return offs[:16].T.reshape(-1).astype(np.int64)


def gelu(v):
    return 0.5 * v * (1.0 + np.tanh(np.sqrt(2.0 / np.pi) * (v + 0.044715 * v**3)))

def planes(y):
    n, m = y.shape
    v = y.astype(np.float32).astype(ml_dtypes.bfloat16).astype(np.float64).reshape(n // 32, 32, m)
    top = np.abs(v).max(1)
    byte = np.clip(np.where(top > 0, np.frexp(top)[1] - 1 + 127 - 7, 1), 1, 254)
    codes = (v * np.exp2(127.0 - byte)[:, None, :]).reshape(n, m).astype(np.float32).astype(ml_dtypes.float8_e4m3fn).view(np.uint8)
    words = codes.reshape(n // 512, 128, 4, m).transpose(0, 1, 3, 2)
    return np.ascontiguousarray(words), np.ascontiguousarray(byte.astype(np.uint8).reshape(n // 512, 16, m))


K, T, S, H, U = 512, 2048, 512, 512, 1024


def setup_inputs():
    n = np.random.standard_normal
    s = mx_kscale(K)[:, None]
    u = mx_kscale(H)
    return {
        "xT": (n((K, T)) * s).astype(np.float32),
        "w1": (n((K, H)) / np.sqrt(K) / s * u).astype(np.float32),
        "w2": (n((H, H)) / np.sqrt(H) / u[:, None]).astype(np.float32),
        "skip": (n((H, U)) * u[:, None]).astype(np.float32),
        "offs": striped(np.random.permutation(T)[:S]),
        "cell": striped(np.random.permutation(U)[:S]),
    }


def reference(xT, w1, w2, skip, offs, cell):
    xq = mxq(f64(xT)[:, unstriped(offs)], 0, "e4m3")
    up = np.zeros((H, U))
    up[:, unstriped(cell)] = gelu(mxq(f64(w1), 0, "e4m3").T @ xq)
    z = up + f64(skip)
    out_0 = mxq(f64(w2), 0, "e4m3").T @ mxq(z, 0, "e4m3")
    return (out_0,) + planes(out_0)

@@ -1,0 +1,255 @@
+from contextlib import ExitStack
+
+import concourse.mybir as mybir
+
+K, T, S, H, U = 512, 2048, 512, 512, 1024
+FLOPS = 2 * K * H * S + 2 * H * H * U
+
+F32 = mybir.dt.float32
+BF16 = mybir.dt.bfloat16
+I32 = mybir.dt.int32
+U32 = mybir.dt.uint32
+U16 = mybir.dt.uint16
+U8 = mybir.dt.uint8
+FP8X4 = mybir.dt.float8_e4m3fn_x4
+ADD = mybir.AluOpType.add
+GELU = mybir.ActivationFunctionType.Gelu_apprx_tanh
+
+P = 128
+PACK = 4
+HALF = S // 2
+UNIT = 128
+UNITS = U // UNIT
+CHUNKS = [(0, 1), (1, 3), (3, 5), (5, 7), (7, 8)]
+BANK = 512
+NEAR = 4
+
+
+def interleave(copy, out, in_):
+    copy(
+        out.rearrange("p (g i) t -> p g t i", i=NEAR),
+        in_.rearrange("p t (g i) -> p g t i", i=NEAR),
+    )
+
+
+def quantize(nc, codes, scales, grouped):
+    nc.vector.quantize_mx(out=codes.bitcast(FP8X4), scales=scales, in_=grouped)
+
+
+def product(nc, out, w_codes, w_scales, t, codes, scales):
+    cols = slice(t * P, (t + 1) * P)
+    nc.tensor.matmul_mx(
+        out=out,
+        lhsT=w_codes[:, cols].bitcast(FP8X4),
+        lhsT_scale=w_scales[:, cols],
+        rhs=codes.bitcast(FP8X4),
+        rhs_scale=scales,
+        start=True,
+        stop=True,
+    )
+
+
+def tile_picked_unet_gelu_lo_kernel(
+    tc, xT, w1, w2, skip, offs, cell, out_0, out_1, out_2
+):
+    nc = tc.nc
+    with ExitStack() as ctx:
+        keep = ctx.enter_context(tc.tile_pool(name="keep", bufs=1))
+        psum = ctx.enter_context(tc.psum_pool(name="psum", bufs=8))
+
+        def held(name, shape, dtype):
+            return keep.tile(shape, dtype, name=name, align_bytes=64)
+
+        def bank():
+            return psum.tile([P, BANK], F32, name="bank")
+
+        offs_sb = keep.tile([P, S // 16], U16, name="offs_sb")
+        cell_sb = keep.tile([P, S // 16], U16, name="cell_sb")
+        w1_raw = held("w1_raw", [P, PACK, H], F32)
+        w2_raw = held("w2_raw", [P, PACK, H], F32)
+        x_rows = [held("x_rows%d" % t, [P, T], F32) for t in range(PACK)]
+        skip_rows = [held("skip_rows%d" % t, [P, U], F32) for t in range(PACK)]
+        up = [held("up%d" % t, [P, U], F32) for t in range(PACK)]
+
+        x_dealt = xT.rearrange("(p t) c -> p t c", t=PACK)
+        skip_dealt = skip.rearrange("(p t) v -> p t v", t=PACK)
+        nc.sync.dma_start(offs_sb[:], offs)
+        nc.sync.dma_start(w1_raw[:], w1.rearrange("(p j) c -> p j c", j=PACK))
+        for t in range(PACK):
+            nc.sync.dma_start(x_rows[t][:], x_dealt[:, t, :])
+        nc.sync.dma_start(cell_sb[:], cell)
+        nc.sync.dma_start(skip_rows[0][:], skip_dealt[:, 0, :])
+        nc.sync.dma_start(w2_raw[:], w2.rearrange("(p j) c -> p j c", j=PACK))
+        for t in range(1, PACK):
+            nc.sync.dma_start(skip_rows[t][:], skip_dealt[:, t, :])
+
+        for t in range(PACK):
+            nc.vector.memset(up[t][:], 0.0)
+        warm = held("warm", [P, 16], F32)
+        nc.scalar.activation(warm[:], up[0][:, 0:16], GELU)
+
+        def weights(name, raw, grouped_tag, codes_tag):
+            grouped = keep.tile([P, PACK * H], BF16, name=name + "_grouped", tag=grouped_tag, align_bytes=64)
+            codes = keep.tile([P, H], U32, name=name + "_codes", tag=codes_tag, align_bytes=64)
+            scales = held(name + "_scales", [P, H], U8)
+            nc.scalar.copy(
+                grouped[:].rearrange("p (t m j) -> p m j t", t=PACK, j=PACK),
+                raw[:].rearrange("p j (m t) -> p m j t", t=PACK),
+            )
+            return codes, scales, grouped
+
+        w1_codes, w1_scales, w1_grouped = weights("w1", w1_raw, "w1_grouped", "turns")
+        quantize(nc, w1_codes[:], w1_scales[:], w1_grouped[:])
+
+        x_grouped = held("x_grouped", [P, S, PACK], BF16)
+        x_codes = held("x_codes", [P, S], U32)
+        x_scales = held("x_scales", [P, S], U8)
+        for t in range(PACK - 1):
+            nc.vector.tensor_copy(x_grouped[:, :, t], x_rows[t][:].indirect(offs_sb[:]))
+        h_first = []
+        for a in range(2):
+            cols = slice(a * HALF, (a + 1) * HALF)
+            entries = slice(a * HALF // 16, (a + 1) * HALF // 16)
+            nc.vector.tensor_copy(
+                x_grouped[:, cols, PACK - 1], x_rows[PACK - 1][:].indirect(offs_sb[:, entries])
+            )
+            quantize(
+                nc, x_codes[:, cols], x_scales[:, cols],
+                x_grouped[:, cols, :].rearrange("p s t -> p (s t)"),
+            )
+            acc = bank()
+            product(nc, acc[:, 0:HALF], w1_codes, w1_scales, 0, x_codes[:, cols], x_scales[:, cols])
+            h_half = held("h_half%d" % a, [P, HALF], F32)
+            nc.scalar.activation(h_half[:], acc[:, 0:HALF], GELU)
+            h_first.append((h_half, entries))
+
+        z_rows = held("z_rows", [P, UNITS, PACK, UNIT], BF16)
+
+        def by_chunk(rows):
+            return rows[:].rearrange("p (c v) -> p c v", v=UNIT)
+
+        for h_half, entries in h_first:
+            nc.vector.tensor_copy(up[0][:].indirect(cell_sb[:, entries]), h_half[:])
+        nc.gpsimd.tensor_tensor(z_rows[:, :, 0, :], by_chunk(up[0]), by_chunk(skip_rows[0]), ADD)
+        for t in range(1, PACK):
+            acc = bank()
+            product(nc, acc[:], w1_codes, w1_scales, t, x_codes[:], x_scales[:])
+            h_rows = held("h_rows%d" % t, [P, S], F32)
+            nc.scalar.activation(h_rows[:], acc[:], GELU)
+            nc.vector.tensor_copy(up[t][:].indirect(cell_sb[:]), h_rows[:])
+            if t < PACK - 1:
+                nc.gpsimd.tensor_tensor(
+                    z_rows[:, :, t, :], by_chunk(up[t]), by_chunk(skip_rows[t]), ADD
+                )
+
+        y_dealt = out_0.rearrange("(p t) v -> p t v", t=PACK)
+        y_words = out_1[0].rearrange("p c r -> p (c r)").bitcast(I32)
+        y_scales = held("y_scales", [P, U], U8)
+        last = PACK - 1
+        stage = {}
+
+        w2_codes, w2_scales, w2_grouped = weights("w2", w2_raw, "turns", "w2_codes")
+
+        def columns(c):
+            return slice(CHUNKS[c][0] * UNIT, CHUNKS[c][1] * UNIT)
+
+        def width(c):
+            return (CHUNKS[c][1] - CHUNKS[c][0]) * UNIT
+
+        def add_last(u0, u1):
+            nc.vector.tensor_tensor(
+                z_rows[:, u0:u1, last, :],
+                by_chunk(up[last])[:, u0:u1, :],
+                by_chunk(skip_rows[last])[:, u0:u1, :],
+                ADD,
+            )
+
+        def group_z(c, copy):
+            u0, u1 = CHUNKS[c]
+            z_grouped = held("z_grouped%d" % c, [P, width(c), PACK], BF16)
+            copy(
+                z_grouped[:].rearrange("p (u g i) t -> p u g t i", u=u1 - u0, i=NEAR),
+                z_rows[:, u0:u1, :, :].rearrange("p u t (g i) -> p u g t i", i=NEAR),
+            )
+            stage["z", c] = z_grouped
+
+        def quantize_z(c):
+            z_codes = held("z_codes%d" % c, [P, width(c)], U32)
+            z_scales = held("z_scales%d" % c, [P, width(c)], U8)
+            quantize(nc, z_codes[:], z_scales[:], stage["z", c][:].rearrange("p v t -> p (v t)"))
+            stage["zq", c] = (z_codes, z_scales)
+
+        def multiply(c):
+            z_codes, z_scales = stage["zq", c]
+            n = width(c)
+            y_rows = held("y_rows%d" % c, [P, PACK * n], F32)
+            for t0 in range(0, PACK, BANK // n):
+                acc = bank()
+                for e in range(BANK // n):
+                    product(
+                        nc, acc[:, e * n : (e + 1) * n], w2_codes, w2_scales,
+                        t0 + e, z_codes[:], z_scales[:],
+                    )
+                nc.scalar.copy(y_rows[:, t0 * n : t0 * n + BANK], acc[:])
+            y_rows = y_rows[:].rearrange("p (t v) -> p t v", t=PACK)
+            nc.sync.dma_start(y_dealt[:, :, columns(c)], y_rows)
+            stage["y", c] = y_rows
+
+        def group_y(c, copy):
+            y_grouped = held("y_grouped%d" % c, [P, width(c), PACK], BF16)
+            interleave(copy, y_grouped[:], stage["y", c])
+            stage["yg", c] = y_grouped
+
+        y_codes = held("y_codes", [P, U], U32)
+
+        def quantize_y(c):
+            quantize(
+                nc, y_codes[:, columns(c)], y_scales[:, columns(c)],
+                stage["yg", c][:].rearrange("p v t -> p (v t)"),
+            )
+
+        def store_words(c0, c1):
+            cols = slice(columns(c0).start, columns(c1).stop)
+            nc.sync.dma_start(y_words[:, cols], y_codes[:, cols].bitcast(I32))
+
+        on_vector, on_scalar = nc.vector.tensor_copy, nc.scalar.copy
+        quantize(nc, w2_codes[:], w2_scales[:], w2_grouped[:])
+        add_last(0, 1)
+        add_last(1, 3)
+        group_z(0, on_vector)
+        group_z(1, on_scalar)
+        add_last(3, 5)
+        quantize_z(0)
+        multiply(0)
+        group_z(2, on_vector)
+        quantize_z(1)
+        multiply(1)
+        add_last(5, 8)
+        quantize_z(2)
+        multiply(2)
+        group_z(3, on_vector)
+        group_z(4, on_vector)
+        quantize_z(3)
+        multiply(3)
+        quantize_z(4)
+        group_y(0, on_vector)
+        group_y(1, on_vector)
+        quantize_y(0)
+        quantize_y(1)
+        multiply(4)
+        store_words(0, 1)
+        group_y(2, on_vector)
+        group_y(3, on_vector)
+        group_y(4, on_scalar)
+        quantize_y(2)
+        store_words(2, 2)
+        quantize_y(3)
+        quantize_y(4)
+        store_words(3, 4)
+
+        scale_rows = out_2[0].bitcast(I32)
+        for q in range(4):
+            queue = nc.sync if q % 2 == 0 else nc.scalar
+            queue.dma_start(
+                scale_rows[4 * q : 4 * q + 4, :], y_scales[32 * q : 32 * q + 4, :].bitcast(I32)
+            )

@@ -1,6 +1,7 @@
 from contextlib import ExitStack
 
 import concourse.mybir as mybir
+from concourse.masks import make_identity
 
 K, T, S, H, U = 512, 2048, 512, 512, 1024
 FLOPS = 2 * K * H * S + 2 * H * H * U
@@ -23,6 +24,7 @@ UNITS = U // UNIT
 CHUNKS = [(0, 1), (1, 3), (3, 5), (5, 7), (7, 8)]
 BANK = 512
 NEAR = 4
+PER_BANK = BANK // UNIT
 
 
 def interleave(copy, out, in_):
@@ -79,12 +81,17 @@ def tile_picked_unet_gelu_lo_kernel(
             nc.sync.dma_start(x_rows[t][:], x_dealt[:, t, :])
         nc.sync.dma_start(cell_sb[:], cell)
         nc.sync.dma_start(skip_rows[0][:], skip_dealt[:, 0, :])
+        nc.sync.dma_start(skip_rows[1][:], skip_dealt[:, 1, :])
+        nc.sync.dma_start(skip_rows[2][:], skip_dealt[:, 2, :])
         nc.sync.dma_start(w2_raw[:], w2.rearrange("(p j) c -> p j c", j=PACK))
-        for t in range(1, PACK):
-            nc.sync.dma_start(skip_rows[t][:], skip_dealt[:, t, :])
+        nc.sync.dma_start(skip_rows[3][:], skip_dealt[:, 3, :])
 
         for t in range(PACK):
             nc.vector.memset(up[t][:], 0.0)
+        ident32 = held("ident32", [P, P], F32)
+        ident16 = held("ident16", [P, P], BF16)
+        make_identity(nc, ident32[:])
+        make_identity(nc, ident16[:])
         warm = held("warm", [P, 16], F32)
         nc.scalar.activation(warm[:], up[0][:, 0:16], GELU)
 
@@ -128,27 +135,62 @@ def tile_picked_unet_gelu_lo_kernel(
         def by_chunk(rows):
             return rows[:].rearrange("p (c v) -> p c v", v=UNIT)
 
-        for h_half, entries in h_first:
-            nc.vector.tensor_copy(up[0][:].indirect(cell_sb[:, entries]), h_half[:])
-        nc.gpsimd.tensor_tensor(z_rows[:, :, 0, :], by_chunk(up[0]), by_chunk(skip_rows[0]), ADD)
+        h_rows = {}
         for t in range(1, PACK):
             acc = bank()
             product(nc, acc[:], w1_codes, w1_scales, t, x_codes[:], x_scales[:])
-            h_rows = held("h_rows%d" % t, [P, S], F32)
-            nc.scalar.activation(h_rows[:], acc[:], GELU)
-            nc.vector.tensor_copy(up[t][:].indirect(cell_sb[:]), h_rows[:])
-            if t < PACK - 1:
-                nc.gpsimd.tensor_tensor(
-                    z_rows[:, :, t, :], by_chunk(up[t]), by_chunk(skip_rows[t]), ADD
+            h_rows[t] = held("h_rows%d" % t, [P, S], F32)
+            nc.scalar.activation(h_rows[t][:], acc[:], GELU)
+
+        w2_codes, w2_scales, w2_grouped = weights("w2", w2_raw, "turns", "w2_codes")
+
+        def turn(acc, rows, half, first):
+            for b in range(PER_BANK):
+                u = half * PER_BANK + b
+                nc.tensor.matmul(
+                    acc[:, b * UNIT : (b + 1) * UNIT],
+                    lhsT=rows[:, u * UNIT : (u + 1) * UNIT],
+                    rhs=ident32[:],
+                    is_transpose=True,
+                    start=first and b == 0,
+                    stop=not first and b == PER_BANK - 1,
                 )
+
+        def turn_skip(t):
+            sums = [bank(), bank()]
+            for half in range(2):
+                turn(sums[half], skip_rows[t], half, True)
+            return sums
+
+        def add_turned(t, sums):
+            for half in range(2):
+                turn(sums[half], up[t], half, False)
+            for half in range(2):
+                z_turned = held("z_turned%d_%d" % (t, half), [P, BANK], BF16)
+                nc.scalar.copy(z_turned[:], sums[half][:])
+                back = psum.tile([P, BANK], BF16, name="bank")
+                for b in range(PER_BANK):
+                    cols = slice(b * UNIT, (b + 1) * UNIT)
+                    nc.tensor.transpose(back[:, cols], z_turned[:, cols], ident16[:])
+                nc.scalar.copy(
+                    z_rows[:, half * PER_BANK : (half + 1) * PER_BANK, t, :],
+                    back[:].rearrange("p (b v) -> p b v", v=UNIT),
+                )
+
+        sums = turn_skip(0)
+        for h_half, entries in h_first:
+            nc.vector.tensor_copy(up[0][:].indirect(cell_sb[:, entries]), h_half[:])
+        for t in range(1, PACK):
+            ahead = turn_skip(t) if t < PACK - 1 else None
+            nc.vector.tensor_copy(up[t][:].indirect(cell_sb[:]), h_rows[t][:])
+            add_turned(t - 1, sums)
+            sums = ahead
 
         y_dealt = out_0.rearrange("(p t) v -> p t v", t=PACK)
         y_words = out_1[0].rearrange("p c r -> p (c r)").bitcast(I32)
         y_scales = held("y_scales", [P, U], U8)
         last = PACK - 1
         stage = {}
-
-        w2_codes, w2_scales, w2_grouped = weights("w2", w2_raw, "turns", "w2_codes")
 
         def columns(c):
             return slice(CHUNKS[c][0] * UNIT, CHUNKS[c][1] * UNIT)

@@ -21,7 +21,9 @@ PACK = 4
 HALF = S // 2
 UNIT = 128
 UNITS = U // UNIT
-CHUNKS = [(0, 1), (1, 3), (3, 5), (5, 7), (7, 8)]
+CHUNKS = [(0, 1), (1, 2), (2, 4), (4, 6), (6, 7), (7, 8)]
+Z_SLOTS = ["z0", "z1", "z0", "z0", "z2", "z1"]
+GROUPS = [(0, 2), (2, 4), (4, 6), (6, 7), (7, 8)]
 BANK = 512
 NEAR = 4
 PER_BANK = BANK // UNIT
@@ -80,11 +82,9 @@ def tile_picked_unet_gelu_lo_kernel(
         for t in range(PACK):
             nc.sync.dma_start(x_rows[t][:], x_dealt[:, t, :])
         nc.sync.dma_start(cell_sb[:], cell)
-        nc.sync.dma_start(skip_rows[0][:], skip_dealt[:, 0, :])
-        nc.sync.dma_start(skip_rows[1][:], skip_dealt[:, 1, :])
-        nc.sync.dma_start(skip_rows[2][:], skip_dealt[:, 2, :])
         nc.sync.dma_start(w2_raw[:], w2.rearrange("(p j) c -> p j c", j=PACK))
-        nc.sync.dma_start(skip_rows[3][:], skip_dealt[:, 3, :])
+        for t in range(PACK):
+            nc.sync.dma_start(skip_rows[t][:], skip_dealt[:, t, :])
 
         for t in range(PACK):
             nc.vector.memset(up[t][:], 0.0)
@@ -139,18 +139,19 @@ def tile_picked_unet_gelu_lo_kernel(
         for t in range(1, PACK):
             acc = bank()
             product(nc, acc[:], w1_codes, w1_scales, t, x_codes[:], x_scales[:])
+            if t == PACK - 1:
+                w2_codes, w2_scales, w2_grouped = weights("w2", w2_raw, "turns", "w2_codes")
+                quantize(nc, w2_codes[:], w2_scales[:], w2_grouped[:])
             h_rows[t] = held("h_rows%d" % t, [P, S], F32)
             nc.scalar.activation(h_rows[t][:], acc[:], GELU)
 
-        w2_codes, w2_scales, w2_grouped = weights("w2", w2_raw, "turns", "w2_codes")
-
-        def turn(acc, rows, half, first):
+        def turn(acc, rows, half, first, ident):
             for b in range(PER_BANK):
                 u = half * PER_BANK + b
                 nc.tensor.matmul(
                     acc[:, b * UNIT : (b + 1) * UNIT],
                     lhsT=rows[:, u * UNIT : (u + 1) * UNIT],
-                    rhs=ident32[:],
+                    rhs=ident[:],
                     is_transpose=True,
                     start=first and b == 0,
                     stop=not first and b == PER_BANK - 1,
@@ -159,14 +160,18 @@ def tile_picked_unet_gelu_lo_kernel(
         def turn_skip(t):
             sums = [bank(), bank()]
             for half in range(2):
-                turn(sums[half], skip_rows[t], half, True)
+                turn(sums[half], skip_rows[t], half, True, ident32)
             return sums
 
         def add_turned(t, sums):
+            ident = ident32
+            if t > 0:
+                ident = keep.tile([P, P], F32, name="ident_late", tag="turned%d_0" % (t - 1), align_bytes=64)
+                nc.scalar.copy(ident[:], ident32[:])
             for half in range(2):
-                turn(sums[half], up[t], half, False)
+                turn(sums[half], up[t], half, False, ident)
             for half in range(2):
-                z_turned = held("z_turned%d_%d" % (t, half), [P, BANK], BF16)
+                z_turned = keep.tile([P, BANK], BF16, name="z_turned", tag="turned%d_%d" % (t, half), align_bytes=64)
                 nc.scalar.copy(z_turned[:], sums[half][:])
                 back = psum.tile([P, BANK], BF16, name="bank")
                 for b in range(PER_BANK):
@@ -208,7 +213,9 @@ def tile_picked_unet_gelu_lo_kernel(
 
         def group_z(c, copy):
             u0, u1 = CHUNKS[c]
-            z_grouped = held("z_grouped%d" % c, [P, width(c), PACK], BF16)
+            z_grouped = keep.tile(
+                [P, width(c), PACK], BF16, name="z_grouped", tag=Z_SLOTS[c], align_bytes=64
+            )
             copy(
                 z_grouped[:].rearrange("p (u g i) t -> p u g t i", u=u1 - u0, i=NEAR),
                 z_rows[:, u0:u1, :, :].rearrange("p u t (g i) -> p u g t i", i=NEAR),
@@ -221,73 +228,85 @@ def tile_picked_unet_gelu_lo_kernel(
             quantize(nc, z_codes[:], z_scales[:], stage["z", c][:].rearrange("p v t -> p (v t)"))
             stage["zq", c] = (z_codes, z_scales)
 
+        y_rows = [
+            held("y_rows%d" % g, [P, PACK, (u1 - u0) * UNIT], F32)
+            for g, (u0, u1) in enumerate(GROUPS)
+        ]
+
         def multiply(c):
             z_codes, z_scales = stage["zq", c]
             n = width(c)
-            y_rows = held("y_rows%d" % c, [P, PACK * n], F32)
-            for t0 in range(0, PACK, BANK // n):
+            g = [u0 <= CHUNKS[c][0] < u1 for u0, u1 in GROUPS].index(True)
+            v0 = (CHUNKS[c][0] - GROUPS[g][0]) * UNIT
+            per_bank = BANK // n
+            for t0 in range(0, PACK, per_bank):
                 acc = bank()
-                for e in range(BANK // n):
+                for e in range(per_bank):
                     product(
                         nc, acc[:, e * n : (e + 1) * n], w2_codes, w2_scales,
                         t0 + e, z_codes[:], z_scales[:],
                     )
-                nc.scalar.copy(y_rows[:, t0 * n : t0 * n + BANK], acc[:])
-            y_rows = y_rows[:].rearrange("p (t v) -> p t v", t=PACK)
-            nc.sync.dma_start(y_dealt[:, :, columns(c)], y_rows)
-            stage["y", c] = y_rows
+                if c == len(CHUNKS) - 1:
+                    y_grouped = held("y_grouped_last", [P, n, PACK], BF16)
+                    nc.scalar.copy(y_grouped[:], acc[:].rearrange("p (t v) -> p v t", t=PACK))
+                    stage["yg", g] = y_grouped
+                part = y_rows[g][:, t0 : t0 + per_bank, v0 : v0 + n]
+                nc.scalar.copy(part, acc[:].rearrange("p (e v) -> p e v", v=n))
+                nc.sync.dma_start(y_dealt[:, t0 : t0 + per_bank, columns(c)], part)
 
-        def group_y(c, copy):
-            y_grouped = held("y_grouped%d" % c, [P, width(c), PACK], BF16)
-            interleave(copy, y_grouped[:], stage["y", c])
-            stage["yg", c] = y_grouped
+        def group_columns(g):
+            return slice(GROUPS[g][0] * UNIT, GROUPS[g][1] * UNIT)
+
+        def group_y(g, copy):
+            y_grouped = held("y_grouped%d" % g, [P, y_rows[g].shape[2], PACK], BF16)
+            interleave(copy, y_grouped[:], y_rows[g][:])
+            stage["yg", g] = y_grouped
 
         y_codes = held("y_codes", [P, U], U32)
 
-        def quantize_y(c):
+        def quantize_y(g):
             quantize(
-                nc, y_codes[:, columns(c)], y_scales[:, columns(c)],
-                stage["yg", c][:].rearrange("p v t -> p (v t)"),
+                nc, y_codes[:, group_columns(g)], y_scales[:, group_columns(g)],
+                stage["yg", g][:].rearrange("p v t -> p (v t)"),
             )
 
-        def store_words(c0, c1):
-            cols = slice(columns(c0).start, columns(c1).stop)
+        def store_words(g0, g1):
+            cols = slice(group_columns(g0).start, group_columns(g1).stop)
             nc.sync.dma_start(y_words[:, cols], y_codes[:, cols].bitcast(I32))
 
         on_vector, on_scalar = nc.vector.tensor_copy, nc.scalar.copy
-        quantize(nc, w2_codes[:], w2_scales[:], w2_grouped[:])
         add_last(0, 1)
-        add_last(1, 3)
-        group_z(0, on_vector)
+        add_last(1, 2)
+        add_last(2, 8)
+        group_z(0, on_scalar)
         group_z(1, on_scalar)
-        add_last(3, 5)
+        group_z(4, on_scalar)
         quantize_z(0)
         multiply(0)
-        group_z(2, on_vector)
         quantize_z(1)
         multiply(1)
-        add_last(5, 8)
+        group_z(2, on_vector)
+        group_z(5, on_vector)
         quantize_z(2)
         multiply(2)
         group_z(3, on_vector)
-        group_z(4, on_vector)
+        quantize_z(4)
         quantize_z(3)
         multiply(3)
-        quantize_z(4)
+        quantize_z(5)
+        multiply(4)
+        multiply(5)
         group_y(0, on_vector)
         group_y(1, on_vector)
         quantize_y(0)
         quantize_y(1)
-        multiply(4)
         store_words(0, 1)
         group_y(2, on_vector)
         group_y(3, on_vector)
-        group_y(4, on_scalar)
         quantize_y(2)
-        store_words(2, 2)
         quantize_y(3)
         quantize_y(4)
-        store_words(3, 4)
+        store_words(2, 4)
 
         scale_rows = out_2[0].bitcast(I32)
         for q in range(4):

@@ -22,10 +22,12 @@ HALF = S // 2
 UNIT = 128
 UNITS = U // UNIT
 CHUNKS = [(0, 1), (1, 2), (2, 4), (4, 6), (6, 7), (7, 8)]
-Z_SLOTS = ["z0", "z1", "z0", "z0", "z2", "z1"]
+Z_SLOTS = ["z0", "z1", "z3", "z0", "z2", "z1"]
+Y_SLOTS = ["z1", "z0", "y2", "y3"]
 GROUPS = [(0, 2), (2, 4), (4, 6), (6, 7), (7, 8)]
 BANK = 512
 NEAR = 4
+TURNED = 2
 PER_BANK = BANK // UNIT
 
 
@@ -72,7 +74,8 @@ def tile_picked_unet_gelu_lo_kernel(
         w1_raw = held("w1_raw", [P, PACK, H], F32)
         w2_raw = held("w2_raw", [P, PACK, H], F32)
         x_rows = [held("x_rows%d" % t, [P, T], F32) for t in range(PACK)]
-        skip_rows = [held("skip_rows%d" % t, [P, U], F32) for t in range(PACK)]
+        skip_rows = [held("skip_rows%d" % t, [P, U], F32) for t in range(TURNED)]
+        skip_early = held("skip_early", [P, PACK - TURNED, BANK], F32)
         up = [held("up%d" % t, [P, U], F32) for t in range(PACK)]
 
         x_dealt = xT.rearrange("(p t) c -> p t c", t=PACK)
@@ -83,8 +86,9 @@ def tile_picked_unet_gelu_lo_kernel(
             nc.sync.dma_start(x_rows[t][:], x_dealt[:, t, :])
         nc.sync.dma_start(cell_sb[:], cell)
         nc.sync.dma_start(w2_raw[:], w2.rearrange("(p j) c -> p j c", j=PACK))
-        for t in range(PACK):
+        for t in range(TURNED):
             nc.sync.dma_start(skip_rows[t][:], skip_dealt[:, t, :])
+        nc.sync.dma_start(skip_early[:], skip_dealt[:, TURNED:, 0:BANK])
 
         for t in range(PACK):
             nc.vector.memset(up[t][:], 0.0)
@@ -113,7 +117,6 @@ def tile_picked_unet_gelu_lo_kernel(
         x_scales = held("x_scales", [P, S], U8)
         for t in range(PACK - 1):
             nc.vector.tensor_copy(x_grouped[:, :, t], x_rows[t][:].indirect(offs_sb[:]))
-        h_first = []
         for a in range(2):
             cols = slice(a * HALF, (a + 1) * HALF)
             entries = slice(a * HALF // 16, (a + 1) * HALF // 16)
@@ -124,11 +127,17 @@ def tile_picked_unet_gelu_lo_kernel(
                 nc, x_codes[:, cols], x_scales[:, cols],
                 x_grouped[:, cols, :].rearrange("p s t -> p (s t)"),
             )
+        h_first = []
+        for pieces in ([(0, UNIT)], [(UNIT, HALF), (HALF, S)]):
+            s0, s1 = pieces[0][0], pieces[-1][1]
             acc = bank()
-            product(nc, acc[:, 0:HALF], w1_codes, w1_scales, 0, x_codes[:, cols], x_scales[:, cols])
-            h_half = held("h_half%d" % a, [P, HALF], F32)
-            nc.scalar.activation(h_half[:], acc[:, 0:HALF], GELU)
-            h_first.append((h_half, entries))
+            for c0, c1 in pieces:
+                product(
+                    nc, acc[:, c0:c1], w1_codes, w1_scales, 0, x_codes[:, c0:c1], x_scales[:, c0:c1]
+                )
+            h_part = held("h_part%d" % s0, [P, s1 - s0], F32)
+            nc.scalar.activation(h_part[:], acc[:, s0:s1], GELU)
+            h_first.append((h_part, slice(s0 // 16, s1 // 16)))
 
         z_rows = held("z_rows", [P, UNITS, PACK, UNIT], BF16)
 
@@ -145,56 +154,55 @@ def tile_picked_unet_gelu_lo_kernel(
             h_rows[t] = held("h_rows%d" % t, [P, S], F32)
             nc.scalar.activation(h_rows[t][:], acc[:], GELU)
 
-        def turn(acc, rows, half, first, ident):
+        def turn(acc, rows, half, first):
             for b in range(PER_BANK):
                 u = half * PER_BANK + b
                 nc.tensor.matmul(
                     acc[:, b * UNIT : (b + 1) * UNIT],
                     lhsT=rows[:, u * UNIT : (u + 1) * UNIT],
-                    rhs=ident[:],
+                    rhs=ident32[:],
                     is_transpose=True,
                     start=first and b == 0,
                     stop=not first and b == PER_BANK - 1,
                 )
 
-        def turn_skip(t):
-            sums = [bank(), bank()]
+        sums = {}
+        for t in range(TURNED):
             for half in range(2):
-                turn(sums[half], skip_rows[t], half, True, ident32)
-            return sums
-
-        def add_turned(t, sums):
-            ident = ident32
-            if t > 0:
-                ident = keep.tile([P, P], F32, name="ident_late", tag="turned%d_0" % (t - 1), align_bytes=64)
-                nc.scalar.copy(ident[:], ident32[:])
+                sums[t, half] = bank()
+                turn(sums[t, half], skip_rows[t], half, True)
+        for h_half, entries in h_first:
+            nc.vector.tensor_copy(up[0][:].indirect(cell_sb[:, entries]), h_half[:])
+        for t in range(1, PACK):
+            nc.vector.tensor_copy(up[t][:].indirect(cell_sb[:]), h_rows[t][:])
+        for t in range(TURNED):
             for half in range(2):
-                turn(sums[half], up[t], half, False, ident)
-            for half in range(2):
-                z_turned = keep.tile([P, BANK], BF16, name="z_turned", tag="turned%d_%d" % (t, half), align_bytes=64)
-                nc.scalar.copy(z_turned[:], sums[half][:])
+                turn(sums[t, half], up[t], half, False)
+        z_turned = {}
+        for half in range(2):
+            for t in range(TURNED):
+                z_turned[t, half] = keep.tile(
+                    [P, BANK], BF16, name="z_turned", tag="turned%d_%d" % (t, half), align_bytes=64
+                )
+                nc.scalar.copy(z_turned[t, half][:], sums[t, half][:])
+        for half in range(2):
+            for t in range(TURNED):
                 back = psum.tile([P, BANK], BF16, name="bank")
                 for b in range(PER_BANK):
                     cols = slice(b * UNIT, (b + 1) * UNIT)
-                    nc.tensor.transpose(back[:, cols], z_turned[:, cols], ident16[:])
+                    nc.tensor.transpose(back[:, cols], z_turned[t, half][:, cols], ident16[:])
                 nc.scalar.copy(
                     z_rows[:, half * PER_BANK : (half + 1) * PER_BANK, t, :],
                     back[:].rearrange("p (b v) -> p b v", v=UNIT),
                 )
-
-        sums = turn_skip(0)
-        for h_half, entries in h_first:
-            nc.vector.tensor_copy(up[0][:].indirect(cell_sb[:, entries]), h_half[:])
-        for t in range(1, PACK):
-            ahead = turn_skip(t) if t < PACK - 1 else None
-            nc.vector.tensor_copy(up[t][:].indirect(cell_sb[:]), h_rows[t][:])
-            add_turned(t - 1, sums)
-            sums = ahead
+        skip_late = keep.tile(
+            [P, PACK - TURNED, BANK], F32, name="skip_late", tag="turned0_0", align_bytes=64
+        )
+        nc.sync.dma_start(skip_late[:], skip_dealt[:, TURNED:, BANK:U])
 
         y_dealt = out_0.rearrange("(p t) v -> p t v", t=PACK)
         y_words = out_1[0].rearrange("p c r -> p (c r)").bitcast(I32)
         y_scales = held("y_scales", [P, U], U8)
-        last = PACK - 1
         stage = {}
 
         def columns(c):
@@ -204,22 +212,30 @@ def tile_picked_unet_gelu_lo_kernel(
             return (CHUNKS[c][1] - CHUNKS[c][0]) * UNIT
 
         def add_last(u0, u1):
-            nc.vector.tensor_tensor(
-                z_rows[:, u0:u1, last, :],
-                by_chunk(up[last])[:, u0:u1, :],
-                by_chunk(skip_rows[last])[:, u0:u1, :],
-                ADD,
-            )
+            rows, s0 = (skip_early, u0) if u0 < PER_BANK else (skip_late, u0 - PER_BANK)
+            for t in range(TURNED, PACK):
+                nc.vector.tensor_tensor(
+                    z_rows[:, u0:u1, t, :],
+                    by_chunk(up[t])[:, u0:u1, :],
+                    rows[:, t - TURNED, s0 * UNIT : (s0 + u1 - u0) * UNIT].rearrange(
+                        "p (c v) -> p c v", v=UNIT
+                    ),
+                    ADD,
+                )
 
-        def group_z(c, copy):
-            u0, u1 = CHUNKS[c]
+        def group_z(c, *copies):
             z_grouped = keep.tile(
                 [P, width(c), PACK], BF16, name="z_grouped", tag=Z_SLOTS[c], align_bytes=64
             )
-            copy(
-                z_grouped[:].rearrange("p (u g i) t -> p u g t i", u=u1 - u0, i=NEAR),
-                z_rows[:, u0:u1, :, :].rearrange("p u t (g i) -> p u g t i", i=NEAR),
-            )
+            share = (CHUNKS[c][1] - CHUNKS[c][0]) // len(copies)
+            for s, copy in enumerate(copies):
+                u0 = CHUNKS[c][0] + s * share
+                copy(
+                    z_grouped[:, s * share * UNIT : (s + 1) * share * UNIT, :].rearrange(
+                        "p (u g i) t -> p u g t i", u=share, i=NEAR
+                    ),
+                    z_rows[:, u0 : u0 + share, :, :].rearrange("p u t (g i) -> p u g t i", i=NEAR),
+                )
             stage["z", c] = z_grouped
 
         def quantize_z(c):
@@ -258,7 +274,9 @@ def tile_picked_unet_gelu_lo_kernel(
             return slice(GROUPS[g][0] * UNIT, GROUPS[g][1] * UNIT)
 
         def group_y(g, copy):
-            y_grouped = held("y_grouped%d" % g, [P, y_rows[g].shape[2], PACK], BF16)
+            y_grouped = keep.tile(
+                [P, y_rows[g].shape[2], PACK], BF16, name="y_grouped", tag=Y_SLOTS[g], align_bytes=64
+            )
             interleave(copy, y_grouped[:], y_rows[g][:])
             stage["yg", g] = y_grouped
 
@@ -275,24 +293,25 @@ def tile_picked_unet_gelu_lo_kernel(
             nc.sync.dma_start(y_words[:, cols], y_codes[:, cols].bitcast(I32))
 
         on_vector, on_scalar = nc.vector.tensor_copy, nc.scalar.copy
-        add_last(0, 1)
-        add_last(1, 2)
-        add_last(2, 8)
+        add_last(0, 2)
+        add_last(2, 4)
         group_z(0, on_scalar)
         group_z(1, on_scalar)
-        group_z(4, on_scalar)
+        group_z(2, on_scalar, on_vector)
         quantize_z(0)
         multiply(0)
         quantize_z(1)
         multiply(1)
-        group_z(2, on_vector)
-        group_z(5, on_vector)
         quantize_z(2)
         multiply(2)
+        add_last(4, 6)
         group_z(3, on_vector)
-        quantize_z(4)
+        add_last(6, 8)
         quantize_z(3)
+        group_z(4, on_scalar)
+        group_z(5, on_vector)
         multiply(3)
+        quantize_z(4)
         quantize_z(5)
         multiply(4)
         multiply(5)
@@ -304,13 +323,14 @@ def tile_picked_unet_gelu_lo_kernel(
         group_y(2, on_vector)
         group_y(3, on_vector)
         quantize_y(2)
+        store_words(2, 2)
         quantize_y(3)
         quantize_y(4)
-        store_words(2, 4)
+        store_words(3, 4)
 
         scale_rows = out_2[0].bitcast(I32)
         for q in range(4):
-            queue = nc.sync if q % 2 == 0 else nc.scalar
+            queue = nc.sync if q == 0 else nc.scalar
             queue.dma_start(
                 scale_rows[4 * q : 4 * q + 4, :], y_scales[32 * q : 32 * q + 4, :].bitcast(I32)
             )

from contextlib import ExitStack

import concourse.mybir as mybir
from concourse.masks import make_identity

K, T, S, H, U = 512, 2048, 512, 512, 1024
FLOPS = 2 * K * H * S + 2 * H * H * U

F32 = mybir.dt.float32
BF16 = mybir.dt.bfloat16
I32 = mybir.dt.int32
U32 = mybir.dt.uint32
U16 = mybir.dt.uint16
U8 = mybir.dt.uint8
FP8X4 = mybir.dt.float8_e4m3fn_x4
ADD = mybir.AluOpType.add
GELU = mybir.ActivationFunctionType.Gelu_apprx_tanh

P = 128
PACK = 4
HALF = S // 2
UNIT = 128
UNITS = U // UNIT
CHUNKS = [(0, 1), (1, 2), (2, 4), (4, 6), (6, 7), (7, 8)]
Z_SLOTS = ["z0", "z1", "z3", "z0", "z2", "z1"]
Y_SLOTS = ["z1", "z0", "y2", "y3"]
GROUPS = [(0, 2), (2, 4), (4, 6), (6, 7), (7, 8)]
BANK = 512
NEAR = 4
TURNED = 2
PER_BANK = BANK // UNIT


def interleave(copy, out, in_):
    copy(
        out.rearrange("p (g i) t -> p g t i", i=NEAR),
        in_.rearrange("p t (g i) -> p g t i", i=NEAR),
    )


def quantize(nc, codes, scales, grouped):
    nc.vector.quantize_mx(out=codes.bitcast(FP8X4), scales=scales, in_=grouped)


def product(nc, out, w_codes, w_scales, t, codes, scales):
    cols = slice(t * P, (t + 1) * P)
    nc.tensor.matmul_mx(
        out=out,
        lhsT=w_codes[:, cols].bitcast(FP8X4),
        lhsT_scale=w_scales[:, cols],
        rhs=codes.bitcast(FP8X4),
        rhs_scale=scales,
        start=True,
        stop=True,
    )


def tile_picked_unet_gelu_lo_kernel(
    tc, xT, w1, w2, skip, offs, cell, out_0, out_1, out_2
):
    nc = tc.nc
    with ExitStack() as ctx:
        keep = ctx.enter_context(tc.tile_pool(name="keep", bufs=1))
        psum = ctx.enter_context(tc.psum_pool(name="psum", bufs=8))

        def held(name, shape, dtype):
            return keep.tile(shape, dtype, name=name, align_bytes=64)

        def bank():
            return psum.tile([P, BANK], F32, name="bank")

        offs_sb = keep.tile([P, S // 16], U16, name="offs_sb")
        cell_sb = keep.tile([P, S // 16], U16, name="cell_sb")
        w1_raw = held("w1_raw", [P, PACK, H], F32)
        w2_raw = held("w2_raw", [P, PACK, H], F32)
        x_rows = [held("x_rows%d" % t, [P, T], F32) for t in range(PACK)]
        skip_rows = [held("skip_rows%d" % t, [P, U], F32) for t in range(TURNED)]
        skip_early = held("skip_early", [P, PACK - TURNED, BANK], F32)
        up = [held("up%d" % t, [P, U], F32) for t in range(PACK)]

        x_dealt = xT.rearrange("(p t) c -> p t c", t=PACK)
        skip_dealt = skip.rearrange("(p t) v -> p t v", t=PACK)
        nc.sync.dma_start(offs_sb[:], offs)
        nc.sync.dma_start(w1_raw[:], w1.rearrange("(p j) c -> p j c", j=PACK))
        for t in range(PACK):
            nc.sync.dma_start(x_rows[t][:], x_dealt[:, t, :])
        nc.sync.dma_start(cell_sb[:], cell)
        nc.sync.dma_start(w2_raw[:], w2.rearrange("(p j) c -> p j c", j=PACK))
        for t in range(TURNED):
            nc.sync.dma_start(skip_rows[t][:], skip_dealt[:, t, :])
        nc.sync.dma_start(skip_early[:], skip_dealt[:, TURNED:, 0:BANK])

        for t in range(PACK):
            nc.vector.memset(up[t][:], 0.0)
        ident32 = held("ident32", [P, P], F32)
        ident16 = held("ident16", [P, P], BF16)
        make_identity(nc, ident32[:])
        make_identity(nc, ident16[:])
        warm = held("warm", [P, 16], F32)
        nc.scalar.activation(warm[:], up[0][:, 0:16], GELU)

        def weights(name, raw, grouped_tag, codes_tag):
            grouped = keep.tile([P, PACK * H], BF16, name=name + "_grouped", tag=grouped_tag, align_bytes=64)
            codes = keep.tile([P, H], U32, name=name + "_codes", tag=codes_tag, align_bytes=64)
            scales = held(name + "_scales", [P, H], U8)
            nc.scalar.copy(
                grouped[:].rearrange("p (t m j) -> p m j t", t=PACK, j=PACK),
                raw[:].rearrange("p j (m t) -> p m j t", t=PACK),
            )
            return codes, scales, grouped

        w1_codes, w1_scales, w1_grouped = weights("w1", w1_raw, "w1_grouped", "turns")
        quantize(nc, w1_codes[:], w1_scales[:], w1_grouped[:])

        x_grouped = held("x_grouped", [P, S, PACK], BF16)
        x_codes = held("x_codes", [P, S], U32)
        x_scales = held("x_scales", [P, S], U8)
        for t in range(PACK - 1):
            nc.vector.tensor_copy(x_grouped[:, :, t], x_rows[t][:].indirect(offs_sb[:]))
        for a in range(2):
            cols = slice(a * HALF, (a + 1) * HALF)
            entries = slice(a * HALF // 16, (a + 1) * HALF // 16)
            nc.vector.tensor_copy(
                x_grouped[:, cols, PACK - 1], x_rows[PACK - 1][:].indirect(offs_sb[:, entries])
            )
            quantize(
                nc, x_codes[:, cols], x_scales[:, cols],
                x_grouped[:, cols, :].rearrange("p s t -> p (s t)"),
            )
        h_first = []
        for pieces in ([(0, UNIT)], [(UNIT, HALF), (HALF, S)]):
            s0, s1 = pieces[0][0], pieces[-1][1]
            acc = bank()
            for c0, c1 in pieces:
                product(
                    nc, acc[:, c0:c1], w1_codes, w1_scales, 0, x_codes[:, c0:c1], x_scales[:, c0:c1]
                )
            h_part = held("h_part%d" % s0, [P, s1 - s0], F32)
            nc.scalar.activation(h_part[:], acc[:, s0:s1], GELU)
            h_first.append((h_part, slice(s0 // 16, s1 // 16)))

        z_rows = held("z_rows", [P, UNITS, PACK, UNIT], BF16)

        def by_chunk(rows):
            return rows[:].rearrange("p (c v) -> p c v", v=UNIT)

        h_rows = {}
        for t in range(1, PACK):
            acc = bank()
            product(nc, acc[:], w1_codes, w1_scales, t, x_codes[:], x_scales[:])
            if t == PACK - 1:
                w2_codes, w2_scales, w2_grouped = weights("w2", w2_raw, "turns", "w2_codes")
                quantize(nc, w2_codes[:], w2_scales[:], w2_grouped[:])
            h_rows[t] = held("h_rows%d" % t, [P, S], F32)
            nc.scalar.activation(h_rows[t][:], acc[:], GELU)

        def turn(acc, rows, half, first):
            for b in range(PER_BANK):
                u = half * PER_BANK + b
                nc.tensor.matmul(
                    acc[:, b * UNIT : (b + 1) * UNIT],
                    lhsT=rows[:, u * UNIT : (u + 1) * UNIT],
                    rhs=ident32[:],
                    is_transpose=True,
                    start=first and b == 0,
                    stop=not first and b == PER_BANK - 1,
                )

        sums = {}
        for t in range(TURNED):
            for half in range(2):
                sums[t, half] = bank()
                turn(sums[t, half], skip_rows[t], half, True)
        for h_half, entries in h_first:
            nc.vector.tensor_copy(up[0][:].indirect(cell_sb[:, entries]), h_half[:])
        for t in range(1, PACK):
            nc.vector.tensor_copy(up[t][:].indirect(cell_sb[:]), h_rows[t][:])
        for t in range(TURNED):
            for half in range(2):
                turn(sums[t, half], up[t], half, False)
        z_turned = {}
        for half in range(2):
            for t in range(TURNED):
                z_turned[t, half] = keep.tile(
                    [P, BANK], BF16, name="z_turned", tag="turned%d_%d" % (t, half), align_bytes=64
                )
                nc.scalar.copy(z_turned[t, half][:], sums[t, half][:])
        for half in range(2):
            for t in range(TURNED):
                back = psum.tile([P, BANK], BF16, name="bank")
                for b in range(PER_BANK):
                    cols = slice(b * UNIT, (b + 1) * UNIT)
                    nc.tensor.transpose(back[:, cols], z_turned[t, half][:, cols], ident16[:])
                nc.scalar.copy(
                    z_rows[:, half * PER_BANK : (half + 1) * PER_BANK, t, :],
                    back[:].rearrange("p (b v) -> p b v", v=UNIT),
                )
        skip_late = keep.tile(
            [P, PACK - TURNED, BANK], F32, name="skip_late", tag="turned0_0", align_bytes=64
        )
        nc.sync.dma_start(skip_late[:], skip_dealt[:, TURNED:, BANK:U])

        y_dealt = out_0.rearrange("(p t) v -> p t v", t=PACK)
        y_words = out_1[0].rearrange("p c r -> p (c r)").bitcast(I32)
        y_scales = held("y_scales", [P, U], U8)
        stage = {}

        def columns(c):
            return slice(CHUNKS[c][0] * UNIT, CHUNKS[c][1] * UNIT)

        def width(c):
            return (CHUNKS[c][1] - CHUNKS[c][0]) * UNIT

        def add_last(u0, u1):
            rows, s0 = (skip_early, u0) if u0 < PER_BANK else (skip_late, u0 - PER_BANK)
            for t in range(TURNED, PACK):
                nc.vector.tensor_tensor(
                    z_rows[:, u0:u1, t, :],
                    by_chunk(up[t])[:, u0:u1, :],
                    rows[:, t - TURNED, s0 * UNIT : (s0 + u1 - u0) * UNIT].rearrange(
                        "p (c v) -> p c v", v=UNIT
                    ),
                    ADD,
                )

        def group_z(c, *copies):
            z_grouped = keep.tile(
                [P, width(c), PACK], BF16, name="z_grouped", tag=Z_SLOTS[c], align_bytes=64
            )
            share = (CHUNKS[c][1] - CHUNKS[c][0]) // len(copies)
            for s, copy in enumerate(copies):
                u0 = CHUNKS[c][0] + s * share
                copy(
                    z_grouped[:, s * share * UNIT : (s + 1) * share * UNIT, :].rearrange(
                        "p (u g i) t -> p u g t i", u=share, i=NEAR
                    ),
                    z_rows[:, u0 : u0 + share, :, :].rearrange("p u t (g i) -> p u g t i", i=NEAR),
                )
            stage["z", c] = z_grouped

        def quantize_z(c):
            z_codes = held("z_codes%d" % c, [P, width(c)], U32)
            z_scales = held("z_scales%d" % c, [P, width(c)], U8)
            quantize(nc, z_codes[:], z_scales[:], stage["z", c][:].rearrange("p v t -> p (v t)"))
            stage["zq", c] = (z_codes, z_scales)

        y_rows = [
            held("y_rows%d" % g, [P, PACK, (u1 - u0) * UNIT], F32)
            for g, (u0, u1) in enumerate(GROUPS)
        ]

        def multiply(c):
            z_codes, z_scales = stage["zq", c]
            n = width(c)
            g = [u0 <= CHUNKS[c][0] < u1 for u0, u1 in GROUPS].index(True)
            v0 = (CHUNKS[c][0] - GROUPS[g][0]) * UNIT
            per_bank = BANK // n
            for t0 in range(0, PACK, per_bank):
                acc = bank()
                for e in range(per_bank):
                    product(
                        nc, acc[:, e * n : (e + 1) * n], w2_codes, w2_scales,
                        t0 + e, z_codes[:], z_scales[:],
                    )
                if c == len(CHUNKS) - 1:
                    y_grouped = held("y_grouped_last", [P, n, PACK], BF16)
                    nc.scalar.copy(y_grouped[:], acc[:].rearrange("p (t v) -> p v t", t=PACK))
                    stage["yg", g] = y_grouped
                part = y_rows[g][:, t0 : t0 + per_bank, v0 : v0 + n]
                nc.scalar.copy(part, acc[:].rearrange("p (e v) -> p e v", v=n))
                nc.sync.dma_start(y_dealt[:, t0 : t0 + per_bank, columns(c)], part)

        def group_columns(g):
            return slice(GROUPS[g][0] * UNIT, GROUPS[g][1] * UNIT)

        def group_y(g, copy):
            y_grouped = keep.tile(
                [P, y_rows[g].shape[2], PACK], BF16, name="y_grouped", tag=Y_SLOTS[g], align_bytes=64
            )
            interleave(copy, y_grouped[:], y_rows[g][:])
            stage["yg", g] = y_grouped

        y_codes = held("y_codes", [P, U], U32)

        def quantize_y(g):
            quantize(
                nc, y_codes[:, group_columns(g)], y_scales[:, group_columns(g)],
                stage["yg", g][:].rearrange("p v t -> p (v t)"),
            )

        def store_words(g0, g1):
            cols = slice(group_columns(g0).start, group_columns(g1).stop)
            nc.sync.dma_start(y_words[:, cols], y_codes[:, cols].bitcast(I32))

        on_vector, on_scalar = nc.vector.tensor_copy, nc.scalar.copy
        add_last(0, 2)
        add_last(2, 4)
        group_z(0, on_scalar)
        group_z(1, on_scalar)
        group_z(2, on_scalar, on_vector)
        quantize_z(0)
        multiply(0)
        quantize_z(1)
        multiply(1)
        quantize_z(2)
        multiply(2)
        add_last(4, 6)
        group_z(3, on_vector)
        add_last(6, 8)
        quantize_z(3)
        group_z(4, on_scalar)
        group_z(5, on_vector)
        multiply(3)
        quantize_z(4)
        quantize_z(5)
        multiply(4)
        multiply(5)
        group_y(0, on_vector)
        group_y(1, on_vector)
        quantize_y(0)
        quantize_y(1)
        store_words(0, 1)
        group_y(2, on_vector)
        group_y(3, on_vector)
        quantize_y(2)
        store_words(2, 2)
        quantize_y(3)
        quantize_y(4)
        store_words(3, 4)

        scale_rows = out_2[0].bitcast(I32)
        for q in range(4):
            queue = nc.sync if q == 0 else nc.scalar
            queue.dma_start(
                scale_rows[4 * q : 4 * q + 4, :], y_scales[32 * q : 32 * q + 4, :].bitcast(I32)
            )
